import numpy as np
import ml_dtypes


def mxq(x, axis, fmt="e4m3"):
    dtype, down = {"e4m3": (ml_dtypes.float8_e4m3fn, 7), "e5m2": (ml_dtypes.float8_e5m2, 14)}[fmt]
    v = np.moveaxis(np.asarray(x, np.float32).astype(ml_dtypes.bfloat16).astype(np.float64), axis, -1)
    blocks = v.reshape(v.shape[:-1] + (-1, 32))
    amax = np.abs(blocks).max(-1, keepdims=True)
    byte = np.maximum(np.where(amax > 0, np.frexp(amax)[1] - 1 + 127, 0) - down, 1)
    scale = np.exp2(byte - 127.0)
    codes = (blocks / scale).astype(np.float32).astype(dtype).astype(np.float64)
    return np.moveaxis((codes * scale).reshape(v.shape), -1, axis)


WIDE = False


def mx_kscale(k):
    if not WIDE:
        return np.ones(k)
    levels = np.array([10, -10, 5, -5, 0])
    if k % 512:
        return np.exp2(np.random.permutation(np.resize(levels, k // 32))).repeat(32)
    a = np.empty((k // 512, 16))
    for p in range(k // 512):
        a[p, :8] = np.random.permutation(np.resize(levels, 8))
        for g in range(8):
            far = levels[np.abs(levels - a[p, g]) >= 10]
            a[p, g + 8] = far[np.random.randint(len(far))]
    return np.exp2(a.ravel()).repeat(32)


def f64(x):
    return np.asarray(x).astype(np.float64)


def striped(idx):
    return np.tile(idx.reshape(-1, 16).T, (8, 1)).astype(np.uint16)


def unstriped(offs):
    return offs[:16].T.reshape(-1).astype(np.int64)


def pack_weight(w):
    k, n = w.shape
    w = f64(np.asarray(w, np.float32).astype(ml_dtypes.bfloat16)).reshape(k // 32, 32, n)
    amax = np.abs(w).max(1)
    byte = np.clip(np.where(amax > 0, np.frexp(amax)[1] - 1 + 127 - 7, 1), 1, 254)
    scaled = (w * np.exp2(127.0 - byte)[:, None, :]).reshape(k, n).astype(np.float32)
    words = np.ascontiguousarray(scaled.reshape(k // 512, 128, 4, n).transpose(0, 1, 3, 2)).astype(ml_dtypes.float8_e4m3fn).view(np.uint8)
    return words, np.ascontiguousarray(byte.astype(np.uint8).reshape(k // 512, 16, n))


def unpack_weight(words, scales):
    g, p, n, _ = words.shape
    vals = np.ascontiguousarray(words).view(ml_dtypes.float8_e4m3fn).astype(np.float64) * np.repeat(np.exp2(scales.astype(np.float64) - 127.0), 8, axis=1)[..., None]
    return vals.transpose(0, 1, 3, 2).reshape(g * 512, n)


def relu(v):
    return np.maximum(v, 0.0)


K, T, D, S, V, N = 1024, 512, 8, 2048, 256, 512


def setup_inputs():
    n = np.random.standard_normal
    s = mx_kscale(K)[:, None]
    words, scales = pack_weight(n((K, N)) / np.sqrt(K) / s)
    return {
        "xT": (n((K, T)) * s).astype(np.float32),
        "w_words": words,
        "w_scales": scales,
        "b": (0.3 * n((N, 1))).astype(np.float32),
        "offs": striped(np.concatenate([np.random.permutation(T)[:V] for _ in range(D)])),
    }


def reference(xT, w_words, w_scales, b, offs):
    w = unpack_weight(w_words, w_scales)
    idx = unstriped(offs)
    x = np.empty((K, V))
    for l in range(D):
        r = l // 4 * (4 * K // D) + l % 4 + 4 * np.arange(K // D)
        x[r] = f64(xT)[r][:, idx[l * V:(l + 1) * V]]
    xq = mxq(x, 0, "e4m3")
    return relu((w.T @ xq) + f64(b))

@@ -1,0 +1,144 @@
+from contextlib import ExitStack
+
+import concourse.mybir as mybir
+from concourse.masks import make_identity
+
+F32 = mybir.dt.float32
+BF16 = mybir.dt.bfloat16
+I32 = mybir.dt.int32
+U32 = mybir.dt.uint32
+U16 = mybir.dt.uint16
+U8 = mybir.dt.uint8
+FP8X4 = mybir.dt.float8_e4m3fn_x4
+COPY = mybir.ActivationFunctionType.Copy
+RELU = mybir.ActivationFunctionType.Relu
+ADD = mybir.AluOpType.add
+MAX = mybir.AluOpType.max
+MULT = mybir.AluOpType.mult
+
+P = 128
+T = 512
+V = 256
+N = 512
+PASSES = 2
+PACK = 4
+M_TILES = N // P
+FLOPS = 2 * PASSES * P * PACK * N * V
+
+
+def tile_picked_grid_lin_relu_sub_l_kernel(tc, xT, w_words, w_scales, b, offs, out):
+    nc = tc.nc
+    with ExitStack() as ctx:
+        keep = ctx.enter_context(tc.tile_pool(name="keep", bufs=1))
+        psum = ctx.enter_context(tc.psum_pool(name="psum", bufs=1))
+
+        lists = keep.tile([P, PASSES * PACK * V // 16], U16, name="lists")
+        tables = [keep.tile([P, T], F32, name=f"table{l}") for l in range(PASSES * PACK)]
+        w_codes = [keep.tile([P, N], U32, name=f"w_codes{a}", align_bytes=64) for a in range(PASSES)]
+        w_bytes = keep.tile([P, N], U8, name="w_bytes", align_bytes=64)
+        x_rows = [keep.tile([P, V, PACK], BF16, name=f"x_rows{a}", align_bytes=64) for a in range(PASSES)]
+        x_codes = [keep.tile([P, V], U32, name=f"x_codes{a}", align_bytes=64) for a in range(PASSES)]
+        x_bytes = [keep.tile([P, V], U8, name=f"x_bytes{a}", align_bytes=64) for a in range(PASSES)]
+        warm = keep.tile([P, 8], F32, name="warm")
+        warm_out = keep.tile([P, 8], F32, name="warm_out")
+        ident = keep.tile([P, P], F32, name="ident")
+        b_rows = keep.tile([P, P], F32, name="b_rows")
+        b_cols = keep.tile([P, M_TILES], F32, name="b_cols")
+
+        levels = xT.rearrange("(a f r) w -> a r f w", a=PASSES, r=PACK)
+
+        nc.vector.memset(b_rows[:], 0.0)
+        nc.vector.memset(w_bytes[:].bitcast(U32), 0)
+        nc.vector.memset(ident[:], 0.0)
+        nc.vector.memset(warm[:], 0.0)
+        def load_scales(queue, q):
+            queue.dma_start(out=w_bytes[32 * q : 32 * q + 8, :].bitcast(I32), in_=w_scales[:, 4 * q : 4 * q + 4, :].bitcast(I32))
+
+        def load_level(l):
+            nc.sync.dma_start(out=tables[l][:], in_=levels[l // PACK, l % PACK])
+
+        def load_w(a):
+            nc.sync.dma_start(out=w_codes[a][:].bitcast(I32), in_=w_words[a].rearrange("p n r -> p (n r)").bitcast(I32))
+
+        load_level(0)
+        nc.sync.dma_start(out=lists[:], in_=offs)
+        for l in (1, 4, 2, 5):
+            load_level(l)
+        load_scales(nc.scalar, 0)
+        load_scales(nc.scalar, 1)
+        load_level(3)
+        load_level(6)
+        load_w(0)
+        load_level(7)
+        load_w(1)
+        nc.scalar.activation(warm_out[:], warm[:], COPY)
+        make_identity(nc, ident[:], nomemset=True)
+        load_scales(nc.gpsimd, 2)
+        load_scales(nc.gpsimd, 3)
+        nc.gpsimd.dma_start(out=b_rows[0:M_TILES, :], in_=b.rearrange("(c p) o -> c (p o)", p=P))
+        turned = psum.tile([P, P], F32, name="turned", tag="acc3_1")
+        nc.tensor.transpose(turned[:], b_rows[:], ident[:])
+
+        def picked(l, table, v0=0, v1=V):
+            return table[:].indirect(lists[:, (l * V + v0) // 16 : (l * V + v1) // 16])
+
+        H = V // 2
+        accs = [[psum.tile([P, H], F32, name=f"acc{c}_{h}", tag=f"acc{c}_{h}") for h in range(2)] for c in range(M_TILES)]
+
+        def quantise(a, v0=0, v1=V):
+            nc.vector.quantize_mx(
+                out=x_codes[a][:, v0:v1].bitcast(FP8X4),
+                scales=x_bytes[a][:, v0:v1],
+                in_=x_rows[a][:, v0:v1, :].rearrange("p v r -> p (v r)"),
+            )
+
+        def multiply(a, c, h):
+            cols = slice(c * P, (c + 1) * P)
+            points = slice(h * H, (h + 1) * H)
+            nc.tensor.matmul_mx(
+                out=accs[c][h][:],
+                lhsT=w_codes[a][:, cols].bitcast(FP8X4),
+                lhsT_scale=w_bytes[4 * a :, cols],
+                rhs=x_codes[a][:, points].bitcast(FP8X4),
+                rhs_scale=x_bytes[a][:, points],
+                start=(a == 0),
+                stop=(a == PASSES - 1),
+            )
+
+        def by_scalar(l):
+            half = keep.tile([P, T], BF16, name=f"half{l}")
+            nc.vector.tensor_copy(half[:], tables[l][:])
+            nc.scalar.activation(x_rows[l // PACK][:, :, l % PACK], picked(l, half), COPY)
+
+        def by_vector(l, v0=0, v1=V):
+            nc.vector.tensor_copy(x_rows[l // PACK][:, v0:v1, l % PACK], picked(l, tables[l], v0, v1))
+
+        by_scalar(0)
+        by_scalar(1)
+        by_vector(4)
+        by_scalar(2)
+        by_vector(5)
+        by_scalar(3)
+        nc.scalar.copy(b_cols[:], turned[:, 0:M_TILES])
+        by_vector(6)
+        quantise(0)
+        for h in range(2):
+            for c in range(M_TILES):
+                multiply(0, c, h)
+        by_vector(7, 0, H)
+        by_vector(7, H, V)
+        quantise(1, 0, H)
+        quantise(1, H, V)
+        results = [keep.tile([P, V], F32, name=f"result{c}") for c in range(M_TILES)]
+        for h in range(2):
+            for c in range(M_TILES):
+                multiply(1, c, h)
+            for c in range(M_TILES):
+                part = results[c][:, h * H : (h + 1) * H]
+                if c % 2 == 0:
+                    nc.scalar.activation(part, accs[c][h][:], RELU, bias=b_cols[:, c : c + 1])
+                else:
+                    nc.vector.tensor_scalar(part, accs[c][h][:], b_cols[:, c : c + 1], 0.0, ADD, MAX)
+        for c in range(M_TILES):
+            queue = nc.scalar if c % 2 == 0 else nc.sync
+            queue.dma_start(out=out[c * P : (c + 1) * P, :], in_=results[c][:])

@@ -62,14 +62,13 @@ def tile_picked_grid_lin_relu_sub_l_kernel(tc, xT, w_words, w_scales, b, offs, o
 
         load_level(0)
         nc.sync.dma_start(out=lists[:], in_=offs)
-        for l in (1, 4, 2, 5):
+        for l in (2, 1, 3, 4):
             load_level(l)
         load_scales(nc.scalar, 0)
         load_scales(nc.scalar, 1)
-        load_level(3)
-        load_level(6)
+        for l in (6, 5, 7):
+            load_level(l)
         load_w(0)
-        load_level(7)
         load_w(1)
         nc.scalar.activation(warm_out[:], warm[:], COPY)
         make_identity(nc, ident[:], nomemset=True)
@@ -105,40 +104,39 @@ def tile_picked_grid_lin_relu_sub_l_kernel(tc, xT, w_words, w_scales, b, offs, o
                 stop=(a == PASSES - 1),
             )
 
-        def by_scalar(l):
+        def cast(l, engine_copy):
             half = keep.tile([P, T], BF16, name=f"half{l}")
-            nc.vector.tensor_copy(half[:], tables[l][:])
+            engine_copy(half[:], tables[l][:])
+            return half
+
+        def by_scalar(l, half):
             nc.scalar.activation(x_rows[l // PACK][:, :, l % PACK], picked(l, half), COPY)
 
         def by_vector(l, v0=0, v1=V):
             nc.vector.tensor_copy(x_rows[l // PACK][:, v0:v1, l % PACK], picked(l, tables[l], v0, v1))
 
-        by_scalar(0)
-        by_scalar(1)
-        by_vector(4)
-        by_scalar(2)
-        by_vector(5)
-        by_scalar(3)
-        nc.scalar.copy(b_cols[:], turned[:, 0:M_TILES])
+        by_scalar(0, cast(0, nc.vector.tensor_copy))
+        by_vector(2)
+        by_scalar(1, cast(1, nc.vector.tensor_copy))
+        by_vector(3, 0, H)
+        by_vector(3, H, V)
+        quantise(0, 0, H)
+        quantise(0, H, V)
+        by_scalar(4, cast(4, nc.scalar.copy))
         by_vector(6)
-        quantise(0)
-        for h in range(2):
-            for c in range(M_TILES):
-                multiply(0, c, h)
+        by_scalar(5, cast(5, nc.vector.tensor_copy))
         by_vector(7, 0, H)
         by_vector(7, H, V)
         quantise(1, 0, H)
         quantise(1, H, V)
-        results = [keep.tile([P, V], F32, name=f"result{c}") for c in range(M_TILES)]
-        for h in range(2):
-            for c in range(M_TILES):
-                multiply(1, c, h)
-            for c in range(M_TILES):
-                part = results[c][:, h * H : (h + 1) * H]
-                if c % 2 == 0:
-                    nc.scalar.activation(part, accs[c][h][:], RELU, bias=b_cols[:, c : c + 1])
-                else:
-                    nc.vector.tensor_scalar(part, accs[c][h][:], b_cols[:, c : c + 1], 0.0, ADD, MAX)
+        nc.scalar.copy(b_cols[:], turned[:, 0:M_TILES])
         for c in range(M_TILES):
-            queue = nc.scalar if c % 2 == 0 else nc.sync
-            queue.dma_start(out=out[c * P : (c + 1) * P, :], in_=results[c][:])
+            for h in range(2):
+                multiply(0, c, h)
+        results = [keep.tile([P, V], F32, name=f"result{c}") for c in range(M_TILES)]
+        for c in range(M_TILES):
+            for h in range(2):
+                multiply(1, c, h)
+            nc.scalar.activation(results[c][:, 0:H], accs[c][0][:], RELU, bias=b_cols[:, c : c + 1])
+            nc.vector.tensor_scalar(results[c][:, H:V], accs[c][1][:], b_cols[:, c : c + 1], 0.0, ADD, MAX)
+            nc.sync.dma_start(out=out[c * P : (c + 1) * P, :], in_=results[c][:])

@@ -62,19 +62,15 @@ def tile_picked_grid_lin_relu_sub_l_kernel(tc, xT, w_words, w_scales, b, offs, o
 
         load_level(0)
         nc.sync.dma_start(out=lists[:], in_=offs)
-        for l in (2, 1, 3, 4):
-            load_level(l)
-        load_scales(nc.scalar, 0)
-        load_scales(nc.scalar, 1)
-        for l in (6, 5, 7):
+        for l in (2, 1, 3, 4, 6, 5, 7):
             load_level(l)
         load_w(0)
+        for q in range(4):
+            load_scales(nc.sync, q)
         load_w(1)
         nc.scalar.activation(warm_out[:], warm[:], COPY)
         make_identity(nc, ident[:], nomemset=True)
-        load_scales(nc.gpsimd, 2)
-        load_scales(nc.gpsimd, 3)
-        nc.gpsimd.dma_start(out=b_rows[0:M_TILES, :], in_=b.rearrange("(c p) o -> c (p o)", p=P))
+        nc.scalar.dma_start(out=b_rows[0:M_TILES, :], in_=b.rearrange("(c p) o -> c (p o)", p=P))
         turned = psum.tile([P, P], F32, name="turned", tag="acc3_1")
         nc.tensor.transpose(turned[:], b_rows[:], ident[:])
 

@@ -57,28 +57,30 @@ def tile_picked_grid_lin_relu_sub_l_kernel(tc, xT, w_words, w_scales, b, offs, o
         def load_level(l):
             nc.sync.dma_start(out=tables[l][:], in_=levels[l // PACK, l % PACK])
 
-        def load_w(a):
-            nc.sync.dma_start(out=w_codes[a][:].bitcast(I32), in_=w_words[a].rearrange("p n r -> p (n r)").bitcast(I32))
+        def load_w(a, m0, m1):
+            nc.sync.dma_start(out=w_codes[a][:, m0:m1].bitcast(I32), in_=w_words[a].rearrange("p n r -> p (n r)").bitcast(I32)[:, m0:m1])
 
         load_level(0)
         nc.sync.dma_start(out=lists[:], in_=offs)
         for l in (2, 1, 3, 4, 6, 5, 7):
             load_level(l)
-        load_w(0)
         for q in range(4):
             load_scales(nc.sync, q)
-        load_w(1)
+        load_w(0, 0, N // 2)
+        load_w(0, N // 2, N)
+        load_w(1, 0, N)
         nc.scalar.activation(warm_out[:], warm[:], COPY)
         make_identity(nc, ident[:], nomemset=True)
         nc.scalar.dma_start(out=b_rows[0:M_TILES, :], in_=b.rearrange("(c p) o -> c (p o)", p=P))
-        turned = psum.tile([P, P], F32, name="turned", tag="acc3_1")
+        turned = psum.tile([P, P], F32, name="turned")
         nc.tensor.transpose(turned[:], b_rows[:], ident[:])
 
         def picked(l, table, v0=0, v1=V):
             return table[:].indirect(lists[:, (l * V + v0) // 16 : (l * V + v1) // 16])
 
         H = V // 2
-        accs = [[psum.tile([P, H], F32, name=f"acc{c}_{h}", tag=f"acc{c}_{h}") for h in range(2)] for c in range(M_TILES)]
+        spans = [[(0, H), (H, V)] if c in (0, M_TILES - 1) else [(0, V)] for c in range(M_TILES)]
+        accs = [[psum.tile([P, v1 - v0], F32, name=f"acc{c}_{v0}") for v0, v1 in spans[c]] for c in range(M_TILES)]
 
         def quantise(a, v0=0, v1=V):
             nc.vector.quantize_mx(
@@ -89,7 +91,7 @@ def tile_picked_grid_lin_relu_sub_l_kernel(tc, xT, w_words, w_scales, b, offs, o
 
         def multiply(a, c, h):
             cols = slice(c * P, (c + 1) * P)
-            points = slice(h * H, (h + 1) * H)
+            points = slice(*spans[c][h])
             nc.tensor.matmul_mx(
                 out=accs[c][h][:],
                 lhsT=w_codes[a][:, cols].bitcast(FP8X4),
@@ -127,12 +129,15 @@ def tile_picked_grid_lin_relu_sub_l_kernel(tc, xT, w_words, w_scales, b, offs, o
         quantise(1, H, V)
         nc.scalar.copy(b_cols[:], turned[:, 0:M_TILES])
         for c in range(M_TILES):
-            for h in range(2):
+            for h in range(len(spans[c])):
                 multiply(0, c, h)
         results = [keep.tile([P, V], F32, name=f"result{c}") for c in range(M_TILES)]
         for c in range(M_TILES):
-            for h in range(2):
+            for h in range(len(spans[c])):
                 multiply(1, c, h)
-            nc.scalar.activation(results[c][:, 0:H], accs[c][0][:], RELU, bias=b_cols[:, c : c + 1])
-            nc.vector.tensor_scalar(results[c][:, H:V], accs[c][1][:], b_cols[:, c : c + 1], 0.0, ADD, MAX)
+            for h, (v0, v1) in enumerate(spans[c]):
+                if (c + h) % 2 == 0:
+                    nc.scalar.activation(results[c][:, v0:v1], accs[c][h][:], RELU, bias=b_cols[:, c : c + 1])
+                else:
+                    nc.vector.tensor_scalar(results[c][:, v0:v1], accs[c][h][:], b_cols[:, c : c + 1], 0.0, ADD, MAX)
             nc.sync.dma_start(out=out[c * P : (c + 1) * P, :], in_=results[c][:])

@@ -43,7 +43,6 @@ def tile_picked_grid_lin_relu_sub_l_kernel(tc, xT, w_words, w_scales, b, offs, o
         warm_out = keep.tile([P, 8], F32, name="warm_out")
         ident = keep.tile([P, P], F32, name="ident")
         b_rows = keep.tile([P, P], F32, name="b_rows")
-        b_cols = keep.tile([P, M_TILES], F32, name="b_cols")
 
         levels = xT.rearrange("(a f r) w -> a r f w", a=PASSES, r=PACK)
 
@@ -62,7 +61,7 @@ def tile_picked_grid_lin_relu_sub_l_kernel(tc, xT, w_words, w_scales, b, offs, o
 
         load_level(0)
         nc.sync.dma_start(out=lists[:], in_=offs)
-        for l in (2, 1, 3, 4, 6, 5, 7):
+        for l in range(1, PASSES * PACK):
             load_level(l)
         for q in range(4):
             load_scales(nc.sync, q)
@@ -108,25 +107,27 @@ def tile_picked_grid_lin_relu_sub_l_kernel(tc, xT, w_words, w_scales, b, offs, o
             return half
 
         def by_scalar(l, half):
-            nc.scalar.activation(x_rows[l // PACK][:, :, l % PACK], picked(l, half), COPY)
+            for v0, v1 in ((0, H), (H, V)):
+                nc.scalar.activation(x_rows[l // PACK][:, v0:v1, l % PACK], picked(l, half, v0, v1), COPY)
 
         def by_vector(l, v0=0, v1=V):
             nc.vector.tensor_copy(x_rows[l // PACK][:, v0:v1, l % PACK], picked(l, tables[l], v0, v1))
 
         by_scalar(0, cast(0, nc.vector.tensor_copy))
-        by_vector(2)
         by_scalar(1, cast(1, nc.vector.tensor_copy))
+        by_vector(2)
         by_vector(3, 0, H)
         by_vector(3, H, V)
         quantise(0, 0, H)
         quantise(0, H, V)
         by_scalar(4, cast(4, nc.scalar.copy))
-        by_vector(6)
         by_scalar(5, cast(5, nc.vector.tensor_copy))
+        by_vector(6)
         by_vector(7, 0, H)
         by_vector(7, H, V)
         quantise(1, 0, H)
         quantise(1, H, V)
+        b_cols = keep.tile([P, M_TILES], F32, name="b_cols", tag="half5")
         nc.scalar.copy(b_cols[:], turned[:, 0:M_TILES])
         for c in range(M_TILES):
             for h in range(len(spans[c])):

@@ -33,7 +33,8 @@ def tile_picked_grid_lin_relu_sub_l_kernel(tc, xT, w_words, w_scales, b, offs, o
         psum = ctx.enter_context(tc.psum_pool(name="psum", bufs=1))
 
         lists = keep.tile([P, PASSES * PACK * V // 16], U16, name="lists")
-        tables = [keep.tile([P, T], F32, name=f"table{l}") for l in range(PASSES * PACK)]
+        first_two = keep.tile([P, 2 * T], F32, name="first_two")
+        tables = [first_two[:, :T], first_two[:, T:]] + [keep.tile([P, T], F32, name=f"table{l}") for l in range(2, PASSES * PACK)]
         w_codes = [keep.tile([P, N], U32, name=f"w_codes{a}", align_bytes=64) for a in range(PASSES)]
         w_bytes = keep.tile([P, N], U8, name="w_bytes", align_bytes=64)
         x_rows = [keep.tile([P, V, PACK], BF16, name=f"x_rows{a}", align_bytes=64) for a in range(PASSES)]
@@ -59,15 +60,16 @@ def tile_picked_grid_lin_relu_sub_l_kernel(tc, xT, w_words, w_scales, b, offs, o
         def load_w(a, m0, m1):
             nc.sync.dma_start(out=w_codes[a][:, m0:m1].bitcast(I32), in_=w_words[a].rearrange("p n r -> p (n r)").bitcast(I32)[:, m0:m1])
 
-        load_level(0)
+        nc.sync.dma_start(out=first_two[:], in_=xT.rearrange("(a f r) w -> a f (r w)", a=PASSES, r=PACK)[0, :, : 2 * T])
         nc.sync.dma_start(out=lists[:], in_=offs)
-        for l in range(1, PASSES * PACK):
+        for l in range(2, PASSES * PACK):
             load_level(l)
         for q in range(4):
             load_scales(nc.sync, q)
         load_w(0, 0, N // 2)
         load_w(0, N // 2, N)
-        load_w(1, 0, N)
+        load_w(1, 0, N // 2)
+        load_w(1, N // 2, N)
         nc.scalar.activation(warm_out[:], warm[:], COPY)
         make_identity(nc, ident[:], nomemset=True)
         nc.scalar.dma_start(out=b_rows[0:M_TILES, :], in_=b.rearrange("(c p) o -> c (p o)", p=P))
@@ -78,7 +80,7 @@ def tile_picked_grid_lin_relu_sub_l_kernel(tc, xT, w_words, w_scales, b, offs, o
             return table[:].indirect(lists[:, (l * V + v0) // 16 : (l * V + v1) // 16])
 
         H = V // 2
-        spans = [[(0, H), (H, V)] if c in (0, M_TILES - 1) else [(0, V)] for c in range(M_TILES)]
+        spans = [[(0, H), (H, V)] if c != 2 else [(0, V)] for c in range(M_TILES)]
         accs = [[psum.tile([P, v1 - v0], F32, name=f"acc{c}_{v0}") for v0, v1 in spans[c]] for c in range(M_TILES)]
 
         def quantise(a, v0=0, v1=V):
@@ -133,12 +135,15 @@ def tile_picked_grid_lin_relu_sub_l_kernel(tc, xT, w_words, w_scales, b, offs, o
             for h in range(len(spans[c])):
                 multiply(0, c, h)
         results = [keep.tile([P, V], F32, name=f"result{c}") for c in range(M_TILES)]
-        for c in range(M_TILES):
-            for h in range(len(spans[c])):
-                multiply(1, c, h)
-            for h, (v0, v1) in enumerate(spans[c]):
-                if (c + h) % 2 == 0:
-                    nc.scalar.activation(results[c][:, v0:v1], accs[c][h][:], RELU, bias=b_cols[:, c : c + 1])
-                else:
-                    nc.vector.tensor_scalar(results[c][:, v0:v1], accs[c][h][:], b_cols[:, c : c + 1], 0.0, ADD, MAX)
-            nc.sync.dma_start(out=out[c * P : (c + 1) * P, :], in_=results[c][:])
+        order = [(0, 0), (1, 0), (0, 1), (1, 1), (2, 0), (3, 0), (3, 1)]
+        for i, (c, h) in enumerate(order):
+            v0, v1 = spans[c][h]
+            multiply(1, c, h)
+            if i % 2 == 0:
+                nc.scalar.activation(results[c][:, v0:v1], accs[c][h][:], RELU, bias=b_cols[:, c : c + 1])
+            else:
+                nc.vector.tensor_scalar(results[c][:, v0:v1], accs[c][h][:], b_cols[:, c : c + 1], 0.0, ADD, MAX)
+            if c < 2:
+                nc.sync.dma_start(out=out[c * P : (c + 1) * P, v0:v1], in_=results[c][:, v0:v1])
+            elif v1 == V:
+                nc.sync.dma_start(out=out[c * P : (c + 1) * P, :], in_=results[c][:])

@@ -108,6 +108,9 @@ def tile_picked_grid_lin_relu_sub_l_kernel(tc, xT, w_words, w_scales, b, offs, o
             engine_copy(half[:], tables[l][:])
             return half
 
+        def round_on_gpsimd(half, table):
+            nc.gpsimd.tensor_scalar(half, table, 1.0, 0.0, MULT, ADD)
+
         def by_scalar(l, half):
             for v0, v1 in ((0, H), (H, V)):
                 nc.scalar.activation(x_rows[l // PACK][:, v0:v1, l % PACK], picked(l, half, v0, v1), COPY)
@@ -122,8 +125,8 @@ def tile_picked_grid_lin_relu_sub_l_kernel(tc, xT, w_words, w_scales, b, offs, o
         by_vector(3, H, V)
         quantise(0, 0, H)
         quantise(0, H, V)
-        by_scalar(4, cast(4, nc.scalar.copy))
-        by_scalar(5, cast(5, nc.vector.tensor_copy))
+        by_scalar(4, cast(4, round_on_gpsimd))
+        by_scalar(5, cast(5, round_on_gpsimd))
         by_vector(6)
         by_vector(7, 0, H)
         by_vector(7, H, V)

@@ -33,8 +33,9 @@ def tile_picked_grid_lin_relu_sub_l_kernel(tc, xT, w_words, w_scales, b, offs, o
         psum = ctx.enter_context(tc.psum_pool(name="psum", bufs=1))
 
         lists = keep.tile([P, PASSES * PACK * V // 16], U16, name="lists")
-        first_two = keep.tile([P, 2 * T], F32, name="first_two")
-        tables = [first_two[:, :T], first_two[:, T:]] + [keep.tile([P, T], F32, name=f"table{l}") for l in range(2, PASSES * PACK)]
+        groups = [(0, 1), (2,), (3,), (4,), (5, 6), (7,)]
+        loaded = [keep.tile([P, len(group), T], F32, name=f"levels{group[0]}") for group in groups]
+        tables = {l: tile[:, i, :] for group, tile in zip(groups, loaded) for i, l in enumerate(group)}
         w_codes = [keep.tile([P, N], U32, name=f"w_codes{a}", align_bytes=64) for a in range(PASSES)]
         w_bytes = keep.tile([P, N], U8, name="w_bytes", align_bytes=64)
         x_rows = [keep.tile([P, V, PACK], BF16, name=f"x_rows{a}", align_bytes=64) for a in range(PASSES)]
@@ -45,39 +46,42 @@ def tile_picked_grid_lin_relu_sub_l_kernel(tc, xT, w_words, w_scales, b, offs, o
         ident = keep.tile([P, P], F32, name="ident")
         b_rows = keep.tile([P, P], F32, name="b_rows")
 
-        levels = xT.rearrange("(a f r) w -> a r f w", a=PASSES, r=PACK)
+        levels = xT.rearrange("(a f r) w -> a f r w", a=PASSES, r=PACK)
 
-        nc.vector.memset(b_rows[:], 0.0)
+        nc.scalar.dma_start(out=b_rows[P - M_TILES :, :], in_=b.rearrange("(c p) o -> c (p o)", p=P))
         nc.vector.memset(w_bytes[:].bitcast(U32), 0)
-        nc.vector.memset(ident[:], 0.0)
         nc.vector.memset(warm[:], 0.0)
-        def load_scales(queue, q):
-            queue.dma_start(out=w_bytes[32 * q : 32 * q + 8, :].bitcast(I32), in_=w_scales[:, 4 * q : 4 * q + 4, :].bitcast(I32))
+        nc.vector.memset(ident[:], 0.0)
+        nc.vector.memset(b_rows[: P - M_TILES, :], 0.0)
 
-        def load_level(l):
-            nc.sync.dma_start(out=tables[l][:], in_=levels[l // PACK, l % PACK])
+        def load_scales():
+            for q in range(4):
+                nc.sync.dma_start(out=w_bytes[32 * q : 32 * q + 8, :].bitcast(I32), in_=w_scales[:, 4 * q : 4 * q + 4, :].bitcast(I32))
+
+        def load_group(i):
+            first, last = groups[i][0] % PACK, groups[i][-1] % PACK
+            step = (last - first) // (len(groups[i]) - 1) if last > first else 1
+            nc.sync.dma_start(out=loaded[i][:], in_=levels[groups[i][0] // PACK, :, first : last + 1 : step, :])
 
         def load_w(a, m0, m1):
             nc.sync.dma_start(out=w_codes[a][:, m0:m1].bitcast(I32), in_=w_words[a].rearrange("p n r -> p (n r)").bitcast(I32)[:, m0:m1])
 
-        nc.sync.dma_start(out=first_two[:], in_=xT.rearrange("(a f r) w -> a f (r w)", a=PASSES, r=PACK)[0, :, : 2 * T])
+        load_group(0)
         nc.sync.dma_start(out=lists[:], in_=offs)
-        for l in range(2, PASSES * PACK):
-            load_level(l)
-        for q in range(4):
-            load_scales(nc.sync, q)
-        load_w(0, 0, N // 2)
-        load_w(0, N // 2, N)
-        load_w(1, 0, N // 2)
-        load_w(1, N // 2, N)
+        for i in range(1, len(groups)):
+            load_group(i)
+        load_scales()
+        for a in range(PASSES):
+            load_w(a, 0, N // 2)
+            load_w(a, N // 2, N)
+
         nc.scalar.activation(warm_out[:], warm[:], COPY)
         make_identity(nc, ident[:], nomemset=True)
-        nc.scalar.dma_start(out=b_rows[0:M_TILES, :], in_=b.rearrange("(c p) o -> c (p o)", p=P))
         turned = psum.tile([P, P], F32, name="turned")
         nc.tensor.transpose(turned[:], b_rows[:], ident[:])
 
-        def picked(l, table, v0=0, v1=V):
-            return table[:].indirect(lists[:, (l * V + v0) // 16 : (l * V + v1) // 16])
+        def picked(l, table, v0, v1):
+            return table.indirect(lists[:, (l * V + v0) // 16 : (l * V + v1) // 16])
 
         H = V // 2
         spans = [[(0, H), (H, V)] if c != 2 else [(0, V)] for c in range(M_TILES)]
@@ -103,50 +107,55 @@ def tile_picked_grid_lin_relu_sub_l_kernel(tc, xT, w_words, w_scales, b, offs, o
                 stop=(a == PASSES - 1),
             )
 
+        halves = {}
+
         def cast(l, engine_copy):
-            half = keep.tile([P, T], BF16, name=f"half{l}")
-            engine_copy(half[:], tables[l][:])
-            return half
+            halves[l] = keep.tile([P, T], BF16, name=f"half{l}")
+            engine_copy(halves[l][:], tables[l])
 
-        def round_on_gpsimd(half, table):
-            nc.gpsimd.tensor_scalar(half, table, 1.0, 0.0, MULT, ADD)
-
-        def by_scalar(l, half):
-            for v0, v1 in ((0, H), (H, V)):
-                nc.scalar.activation(x_rows[l // PACK][:, v0:v1, l % PACK], picked(l, half, v0, v1), COPY)
+        def by_scalar(l, v0=0, v1=V):
+            nc.scalar.activation(x_rows[l // PACK][:, v0:v1, l % PACK], picked(l, halves[l][:], v0, v1), COPY)
 
         def by_vector(l, v0=0, v1=V):
             nc.vector.tensor_copy(x_rows[l // PACK][:, v0:v1, l % PACK], picked(l, tables[l], v0, v1))
 
-        by_scalar(0, cast(0, nc.vector.tensor_copy))
-        by_scalar(1, cast(1, nc.vector.tensor_copy))
+        def round_on_gpsimd(half, table):
+            nc.gpsimd.tensor_scalar(half, table, 1.0, 0.0, MULT, ADD)
+
+        cast(0, nc.vector.tensor_copy)
+        cast(1, nc.vector.tensor_copy)
+        by_scalar(0)
+        by_scalar(1)
         by_vector(2)
-        by_vector(3, 0, H)
-        by_vector(3, H, V)
-        quantise(0, 0, H)
-        quantise(0, H, V)
-        by_scalar(4, cast(4, round_on_gpsimd))
-        by_scalar(5, cast(5, round_on_gpsimd))
+        by_vector(3)
+        quantise(0)
+        cast(4, nc.scalar.copy)
+        cast(5, round_on_gpsimd)
+        by_scalar(4)
+        by_scalar(5, 0, H)
+        by_scalar(5, H, V)
         by_vector(6)
         by_vector(7, 0, H)
         by_vector(7, H, V)
         quantise(1, 0, H)
         quantise(1, H, V)
+
         b_cols = keep.tile([P, M_TILES], F32, name="b_cols", tag="half5")
-        nc.scalar.copy(b_cols[:], turned[:, 0:M_TILES])
+        nc.scalar.copy(b_cols[:], turned[:, P - M_TILES :])
         for c in range(M_TILES):
             for h in range(len(spans[c])):
                 multiply(0, c, h)
-        results = [keep.tile([P, V], F32, name=f"result{c}") for c in range(M_TILES)]
+        results = keep.tile([P, M_TILES, V], F32, name="results")
+        out_tiles = out.rearrange("(c p) v -> p c v", p=P)
         order = [(0, 0), (1, 0), (0, 1), (1, 1), (2, 0), (3, 0), (3, 1)]
+        stores = {(0, 0): (0, 1, 0, H), (1, 0): (1, 2, 0, H), (1, 1): (0, 2, H, V), (2, 0): (2, 3, 0, V), (3, 1): (3, 4, 0, V)}
         for i, (c, h) in enumerate(order):
             v0, v1 = spans[c][h]
             multiply(1, c, h)
             if i % 2 == 0:
-                nc.scalar.activation(results[c][:, v0:v1], accs[c][h][:], RELU, bias=b_cols[:, c : c + 1])
+                nc.scalar.activation(results[:, c, v0:v1], accs[c][h][:], RELU, bias=b_cols[:, c : c + 1])
             else:
-                nc.vector.tensor_scalar(results[c][:, v0:v1], accs[c][h][:], b_cols[:, c : c + 1], 0.0, ADD, MAX)
-            if c < 2:
-                nc.sync.dma_start(out=out[c * P : (c + 1) * P, v0:v1], in_=results[c][:, v0:v1])
-            elif v1 == V:
-                nc.sync.dma_start(out=out[c * P : (c + 1) * P, :], in_=results[c][:])
+                nc.vector.tensor_scalar(results[:, c, v0:v1], accs[c][h][:], b_cols[:, c : c + 1], 0.0, ADD, MAX)
+            if (c, h) in stores:
+                c0, c1, s0, s1 = stores[c, h]
+                nc.sync.dma_start(out=out_tiles[:, c0:c1, s0:s1], in_=results[:, c0:c1, s0:s1])

@@ -33,7 +33,7 @@ def tile_picked_grid_lin_relu_sub_l_kernel(tc, xT, w_words, w_scales, b, offs, o
         psum = ctx.enter_context(tc.psum_pool(name="psum", bufs=1))
 
         lists = keep.tile([P, PASSES * PACK * V // 16], U16, name="lists")
-        groups = [(0, 1), (2,), (3,), (4,), (5, 6), (7,)]
+        groups = [(0, 1), (2,), (3,), (4,), (5,), (6,), (7,)]
         loaded = [keep.tile([P, len(group), T], F32, name=f"levels{group[0]}") for group in groups]
         tables = {l: tile[:, i, :] for group, tile in zip(groups, loaded) for i, l in enumerate(group)}
         w_codes = [keep.tile([P, N], U32, name=f"w_codes{a}", align_bytes=64) for a in range(PASSES)]
@@ -49,13 +49,13 @@ def tile_picked_grid_lin_relu_sub_l_kernel(tc, xT, w_words, w_scales, b, offs, o
         levels = xT.rearrange("(a f r) w -> a f r w", a=PASSES, r=PACK)
 
         nc.scalar.dma_start(out=b_rows[P - M_TILES :, :], in_=b.rearrange("(c p) o -> c (p o)", p=P))
-        nc.vector.memset(w_bytes[:].bitcast(U32), 0)
+        nc.gpsimd.memset(w_bytes[:].bitcast(U32), 0)
         nc.vector.memset(warm[:], 0.0)
         nc.vector.memset(ident[:], 0.0)
         nc.vector.memset(b_rows[: P - M_TILES, :], 0.0)
 
-        def load_scales():
-            for q in range(4):
+        def load_scales(q0, q1):
+            for q in range(q0, q1):
                 nc.sync.dma_start(out=w_bytes[32 * q : 32 * q + 8, :].bitcast(I32), in_=w_scales[:, 4 * q : 4 * q + 4, :].bitcast(I32))
 
         def load_group(i):
@@ -68,12 +68,15 @@ def tile_picked_grid_lin_relu_sub_l_kernel(tc, xT, w_words, w_scales, b, offs, o
 
         load_group(0)
         nc.sync.dma_start(out=lists[:], in_=offs)
-        for i in range(1, len(groups)):
+        for i in range(1, len(groups) - 1):
             load_group(i)
-        load_scales()
-        for a in range(PASSES):
-            load_w(a, 0, N // 2)
-            load_w(a, N // 2, N)
+        load_scales(0, 2)
+        load_group(len(groups) - 1)
+        load_scales(2, 4)
+        load_w(0, 0, N // 2)
+        load_w(0, N // 2, N)
+        load_w(1, N // 2, N)
+        load_w(1, 0, N // 2)
 
         nc.scalar.activation(warm_out[:], warm[:], COPY)
         make_identity(nc, ident[:], nomemset=True)
@@ -84,8 +87,8 @@ def tile_picked_grid_lin_relu_sub_l_kernel(tc, xT, w_words, w_scales, b, offs, o
             return table.indirect(lists[:, (l * V + v0) // 16 : (l * V + v1) // 16])
 
         H = V // 2
-        spans = [[(0, H), (H, V)] if c != 2 else [(0, V)] for c in range(M_TILES)]
-        accs = [[psum.tile([P, v1 - v0], F32, name=f"acc{c}_{v0}") for v0, v1 in spans[c]] for c in range(M_TILES)]
+        spans = [[(0, H), (H, V)] for c in range(M_TILES)]
+        accs = {}
 
         def quantise(a, v0=0, v1=V):
             nc.vector.quantize_mx(
@@ -97,8 +100,11 @@ def tile_picked_grid_lin_relu_sub_l_kernel(tc, xT, w_words, w_scales, b, offs, o
         def multiply(a, c, h):
             cols = slice(c * P, (c + 1) * P)
             points = slice(*spans[c][h])
+            if a == 0:
+                bank = f"bank{c}_0" if c >= 2 and h == 1 else f"bank{c}_{h}"
+                accs[c, h] = psum.tile([P, H], F32, name=f"acc{c}_{h}", tag=bank)
             nc.tensor.matmul_mx(
-                out=accs[c][h][:],
+                out=accs[c, h][:],
                 lhsT=w_codes[a][:, cols].bitcast(FP8X4),
                 lhsT_scale=w_bytes[4 * a :, cols],
                 rhs=x_codes[a][:, points].bitcast(FP8X4),
@@ -119,43 +125,52 @@ def tile_picked_grid_lin_relu_sub_l_kernel(tc, xT, w_words, w_scales, b, offs, o
         def by_vector(l, v0=0, v1=V):
             nc.vector.tensor_copy(x_rows[l // PACK][:, v0:v1, l % PACK], picked(l, tables[l], v0, v1))
 
-        def round_on_gpsimd(half, table):
-            nc.gpsimd.tensor_scalar(half, table, 1.0, 0.0, MULT, ADD)
-
         cast(0, nc.vector.tensor_copy)
         cast(1, nc.vector.tensor_copy)
         by_scalar(0)
-        by_scalar(1)
+        by_scalar(1, 0, H)
+        by_scalar(1, H, V)
         by_vector(2)
-        by_vector(3)
-        quantise(0)
+        by_vector(3, 0, H)
+        by_vector(3, H, V)
+        quantise(0, 0, H)
+        quantise(0, H, V)
         cast(4, nc.scalar.copy)
-        cast(5, round_on_gpsimd)
-        by_scalar(4)
-        by_scalar(5, 0, H)
-        by_scalar(5, H, V)
+        cast(5, nc.vector.tensor_copy)
+        for v0, v1 in ((0, H), (H, V)):
+            by_scalar(4, v0, v1)
+            by_scalar(5, v0, v1)
         by_vector(6)
         by_vector(7, 0, H)
-        by_vector(7, H, V)
+        by_vector(7, H, H + 64)
         quantise(1, 0, H)
+        by_vector(7, H + 64, V)
         quantise(1, H, V)
 
-        b_cols = keep.tile([P, M_TILES], F32, name="b_cols", tag="half5")
+        b_cols = keep.tile([P, M_TILES], F32, name="b_cols")
         nc.scalar.copy(b_cols[:], turned[:, P - M_TILES :])
-        for c in range(M_TILES):
-            for h in range(len(spans[c])):
-                multiply(0, c, h)
         results = keep.tile([P, M_TILES, V], F32, name="results")
         out_tiles = out.rearrange("(c p) v -> p c v", p=P)
-        order = [(0, 0), (1, 0), (0, 1), (1, 1), (2, 0), (3, 0), (3, 1)]
-        stores = {(0, 0): (0, 1, 0, H), (1, 0): (1, 2, 0, H), (1, 1): (0, 2, H, V), (2, 0): (2, 3, 0, V), (3, 1): (3, 4, 0, V)}
-        for i, (c, h) in enumerate(order):
+        stores = {(2, 0): (2, 3, 0, H), (3, 0): (3, 4, 0, H), (1, 0): (0, 2, 0, H), (1, 1): (0, 2, H, V), (2, 1): (2, 3, H, V), (3, 1): (3, 4, H, V)}
+        closed = []
+
+        def close(c, h):
             v0, v1 = spans[c][h]
             multiply(1, c, h)
-            if i % 2 == 0:
-                nc.scalar.activation(results[:, c, v0:v1], accs[c][h][:], RELU, bias=b_cols[:, c : c + 1])
+            if len(closed) % 2 == 0:
+                nc.scalar.activation(results[:, c, v0:v1], accs[c, h][:], RELU, bias=b_cols[:, c : c + 1])
             else:
-                nc.vector.tensor_scalar(results[:, c, v0:v1], accs[c][h][:], b_cols[:, c : c + 1], 0.0, ADD, MAX)
+                nc.vector.tensor_scalar(results[:, c, v0:v1], accs[c, h][:], b_cols[:, c : c + 1], 0.0, ADD, MAX)
+            closed.append((c, h))
             if (c, h) in stores:
                 c0, c1, s0, s1 = stores[c, h]
                 nc.sync.dma_start(out=out_tiles[:, c0:c1, s0:s1], in_=results[:, c0:c1, s0:s1])
+
+        for c, h in ((0, 0), (1, 0), (0, 1), (1, 1), (2, 0), (3, 0)):
+            multiply(0, c, h)
+        for c in (2, 3, 0, 1):
+            close(c, 0)
+        for c in range(M_TILES):
+            if c >= 2:
+                multiply(0, c, 1)
+            close(c, 1)

@@ -151,7 +151,7 @@ def tile_picked_grid_lin_relu_sub_l_kernel(tc, xT, w_words, w_scales, b, offs, o
         nc.scalar.copy(b_cols[:], turned[:, P - M_TILES :])
         results = keep.tile([P, M_TILES, V], F32, name="results")
         out_tiles = out.rearrange("(c p) v -> p c v", p=P)
-        stores = {(2, 0): (2, 3, 0, H), (3, 0): (3, 4, 0, H), (1, 0): (0, 2, 0, H), (1, 1): (0, 2, H, V), (2, 1): (2, 3, H, V), (3, 1): (3, 4, H, V)}
+        stores = {(2, 0): (2, 3, 0, H), (3, 0): (3, 4, 0, H), (0, 1): (0, 1, 0, V), (1, 1): (1, 2, 0, V), (2, 1): (2, 3, H, V), (3, 1): (3, 4, H, V)}
         closed = []
 
         def close(c, h):
@@ -168,9 +168,8 @@ def tile_picked_grid_lin_relu_sub_l_kernel(tc, xT, w_words, w_scales, b, offs, o
 
         for c, h in ((0, 0), (1, 0), (0, 1), (1, 1), (2, 0), (3, 0)):
             multiply(0, c, h)
-        for c in (2, 3, 0, 1):
-            close(c, 0)
-        for c in range(M_TILES):
-            if c >= 2:
-                multiply(0, c, 1)
+        for c, h in ((2, 0), (3, 0), (0, 0), (0, 1), (1, 0), (1, 1)):
+            close(c, h)
+        for c in (2, 3):
+            multiply(0, c, 1)
             close(c, 1)

@@ -14,15 +14,20 @@ COPY = mybir.ActivationFunctionType.Copy
 RELU = mybir.ActivationFunctionType.Relu
 ADD = mybir.AluOpType.add
 MAX = mybir.AluOpType.max
-MULT = mybir.AluOpType.mult
 
 P = 128
 T = 512
 V = 256
+H = V // 2
+QUARTER = V // 4
 N = 512
 PASSES = 2
 PACK = 4
 M_TILES = N // P
+STRIPE = 16
+QUADRANT = 32
+SCALE_ROWS = 4
+HALVES = ((0, H), (H, V))
 FLOPS = 2 * PASSES * P * PACK * N * V
 
 
@@ -32,8 +37,8 @@ def tile_picked_grid_lin_relu_sub_l_kernel(tc, xT, w_words, w_scales, b, offs, o
         keep = ctx.enter_context(tc.tile_pool(name="keep", bufs=1))
         psum = ctx.enter_context(tc.psum_pool(name="psum", bufs=1))
 
-        lists = keep.tile([P, PASSES * PACK * V // 16], U16, name="lists")
-        groups = [(0, 1), (2,), (3,), (4,), (5,), (6,), (7,)]
+        lists = keep.tile([P, PASSES * PACK * V // STRIPE], U16, name="lists")
+        groups = [(0, 1)] + [(l,) for l in range(2, PASSES * PACK)]
         loaded = [keep.tile([P, len(group), T], F32, name=f"levels{group[0]}") for group in groups]
         tables = {l: tile[:, i, :] for group, tile in zip(groups, loaded) for i, l in enumerate(group)}
         w_codes = [keep.tile([P, N], U32, name=f"w_codes{a}", align_bytes=64) for a in range(PASSES)]
@@ -56,12 +61,14 @@ def tile_picked_grid_lin_relu_sub_l_kernel(tc, xT, w_words, w_scales, b, offs, o
 
         def load_scales(q0, q1):
             for q in range(q0, q1):
-                nc.sync.dma_start(out=w_bytes[32 * q : 32 * q + 8, :].bitcast(I32), in_=w_scales[:, 4 * q : 4 * q + 4, :].bitcast(I32))
+                nc.sync.dma_start(
+                    out=w_bytes[QUADRANT * q : QUADRANT * q + PASSES * SCALE_ROWS, :].bitcast(I32),
+                    in_=w_scales[:, SCALE_ROWS * q : SCALE_ROWS * (q + 1), :].bitcast(I32),
+                )
 
         def load_group(i):
-            first, last = groups[i][0] % PACK, groups[i][-1] % PACK
-            step = (last - first) // (len(groups[i]) - 1) if last > first else 1
-            nc.sync.dma_start(out=loaded[i][:], in_=levels[groups[i][0] // PACK, :, first : last + 1 : step, :])
+            first, last = groups[i][0], groups[i][-1]
+            nc.sync.dma_start(out=loaded[i][:], in_=levels[first // PACK, :, first % PACK : last % PACK + 1, :])
 
         def load_w(a, m0, m1):
             nc.sync.dma_start(out=w_codes[a][:, m0:m1].bitcast(I32), in_=w_words[a].rearrange("p n r -> p (n r)").bitcast(I32)[:, m0:m1])
@@ -83,14 +90,23 @@ def tile_picked_grid_lin_relu_sub_l_kernel(tc, xT, w_words, w_scales, b, offs, o
         turned = psum.tile([P, P], F32, name="turned")
         nc.tensor.transpose(turned[:], b_rows[:], ident[:])
 
-        def picked(l, table, v0, v1):
-            return table.indirect(lists[:, (l * V + v0) // 16 : (l * V + v1) // 16])
-
-        H = V // 2
-        spans = [[(0, H), (H, V)] for c in range(M_TILES)]
+        rounded = {}
         accs = {}
 
-        def quantise(a, v0=0, v1=V):
+        def picked(l, window, v0, v1):
+            return window.indirect(lists[:, (l * V + v0) // STRIPE : (l * V + v1) // STRIPE])
+
+        def cast(l, engine_copy):
+            rounded[l] = keep.tile([P, T], BF16, name=f"half{l}")
+            engine_copy(rounded[l][:], tables[l])
+
+        def by_scalar(l, v0=0, v1=V):
+            nc.scalar.activation(x_rows[l // PACK][:, v0:v1, l % PACK], picked(l, rounded[l][:], v0, v1), COPY)
+
+        def by_vector(l, v0=0, v1=V):
+            nc.vector.tensor_copy(x_rows[l // PACK][:, v0:v1, l % PACK], picked(l, tables[l], v0, v1))
+
+        def quantise(a, v0, v1):
             nc.vector.quantize_mx(
                 out=x_codes[a][:, v0:v1].bitcast(FP8X4),
                 scales=x_bytes[a][:, v0:v1],
@@ -99,77 +115,74 @@ def tile_picked_grid_lin_relu_sub_l_kernel(tc, xT, w_words, w_scales, b, offs, o
 
         def multiply(a, c, h):
             cols = slice(c * P, (c + 1) * P)
-            points = slice(*spans[c][h])
+            points = slice(*HALVES[h])
             if a == 0:
-                bank = f"bank{c}_0" if c >= 2 and h == 1 else f"bank{c}_{h}"
+                bank = f"bank{c}_0" if c >= 2 else f"bank{c}_{h}"
                 accs[c, h] = psum.tile([P, H], F32, name=f"acc{c}_{h}", tag=bank)
             nc.tensor.matmul_mx(
                 out=accs[c, h][:],
                 lhsT=w_codes[a][:, cols].bitcast(FP8X4),
-                lhsT_scale=w_bytes[4 * a :, cols],
+                lhsT_scale=w_bytes[SCALE_ROWS * a :, cols],
                 rhs=x_codes[a][:, points].bitcast(FP8X4),
                 rhs_scale=x_bytes[a][:, points],
                 start=(a == 0),
                 stop=(a == PASSES - 1),
             )
 
-        halves = {}
-
-        def cast(l, engine_copy):
-            halves[l] = keep.tile([P, T], BF16, name=f"half{l}")
-            engine_copy(halves[l][:], tables[l])
-
-        def by_scalar(l, v0=0, v1=V):
-            nc.scalar.activation(x_rows[l // PACK][:, v0:v1, l % PACK], picked(l, halves[l][:], v0, v1), COPY)
-
-        def by_vector(l, v0=0, v1=V):
-            nc.vector.tensor_copy(x_rows[l // PACK][:, v0:v1, l % PACK], picked(l, tables[l], v0, v1))
-
         cast(0, nc.vector.tensor_copy)
         cast(1, nc.vector.tensor_copy)
         by_scalar(0)
-        by_scalar(1, 0, H)
-        by_scalar(1, H, V)
+        for v0, v1 in HALVES:
+            by_scalar(1, v0, v1)
         by_vector(2)
-        by_vector(3, 0, H)
-        by_vector(3, H, V)
-        quantise(0, 0, H)
-        quantise(0, H, V)
+        for v0, v1 in HALVES:
+            by_vector(3, v0, v1)
+        for v0, v1 in HALVES:
+            quantise(0, v0, v1)
+
         cast(4, nc.scalar.copy)
         cast(5, nc.vector.tensor_copy)
-        for v0, v1 in ((0, H), (H, V)):
+        for v0, v1 in HALVES:
             by_scalar(4, v0, v1)
             by_scalar(5, v0, v1)
         by_vector(6)
         by_vector(7, 0, H)
-        by_vector(7, H, H + 64)
+        by_vector(7, H, H + QUARTER)
         quantise(1, 0, H)
-        by_vector(7, H + 64, V)
+        by_vector(7, H + QUARTER, V)
         quantise(1, H, V)
 
         b_cols = keep.tile([P, M_TILES], F32, name="b_cols")
-        nc.scalar.copy(b_cols[:], turned[:, P - M_TILES :])
+        nc.vector.tensor_copy(b_cols[:], turned[:, P - M_TILES :])
         results = keep.tile([P, M_TILES, V], F32, name="results")
         out_tiles = out.rearrange("(c p) v -> p c v", p=P)
-        stores = {(2, 0): (2, 3, 0, H), (3, 0): (3, 4, 0, H), (0, 1): (0, 1, 0, V), (1, 1): (1, 2, 0, V), (2, 1): (2, 3, H, V), (3, 1): (3, 4, H, V)}
         closed = []
 
         def close(c, h):
-            v0, v1 = spans[c][h]
+            v0, v1 = HALVES[h]
             multiply(1, c, h)
             if len(closed) % 2 == 0:
                 nc.scalar.activation(results[:, c, v0:v1], accs[c, h][:], RELU, bias=b_cols[:, c : c + 1])
             else:
                 nc.vector.tensor_scalar(results[:, c, v0:v1], accs[c, h][:], b_cols[:, c : c + 1], 0.0, ADD, MAX)
             closed.append((c, h))
-            if (c, h) in stores:
-                c0, c1, s0, s1 = stores[c, h]
-                nc.sync.dma_start(out=out_tiles[:, c0:c1, s0:s1], in_=results[:, c0:c1, s0:s1])
 
-        for c, h in ((0, 0), (1, 0), (0, 1), (1, 1), (2, 0), (3, 0)):
-            multiply(0, c, h)
-        for c, h in ((2, 0), (3, 0), (0, 0), (0, 1), (1, 0), (1, 1)):
-            close(c, h)
+        def store(c, v0, v1):
+            nc.sync.dma_start(out=out_tiles[:, c : c + 1, v0:v1], in_=results[:, c : c + 1, v0:v1])
+
+        for h in range(2):
+            for c in (0, 1):
+                multiply(0, c, h)
+        for c in (2, 3):
+            multiply(0, c, 0)
+        for c in (2, 3):
+            close(c, 0)
+            store(c, 0, H)
+        for c in (0, 1):
+            for h in range(2):
+                close(c, h)
+            store(c, 0, V)
         for c in (2, 3):
             multiply(0, c, 1)
             close(c, 1)
+            store(c, H, V)

@@ -75,9 +75,11 @@ def tile_picked_grid_lin_relu_sub_l_kernel(tc, xT, w_words, w_scales, b, offs, o
 
         load_group(0)
         nc.sync.dma_start(out=lists[:], in_=offs)
-        for i in range(1, len(groups) - 1):
+        for i in range(1, len(groups) - 2):
             load_group(i)
-        load_scales(0, 2)
+        load_scales(0, 1)
+        load_group(len(groups) - 2)
+        load_scales(1, 2)
         load_group(len(groups) - 1)
         load_scales(2, 4)
         load_w(0, 0, N // 2)

@@ -19,7 +19,6 @@ P = 128
 T = 512
 V = 256
 H = V // 2
-QUARTER = V // 4
 N = 512
 PASSES = 2
 PACK = 4
@@ -38,12 +37,12 @@ def tile_picked_grid_lin_relu_sub_l_kernel(tc, xT, w_words, w_scales, b, offs, o
         psum = ctx.enter_context(tc.psum_pool(name="psum", bufs=1))
 
         lists = keep.tile([P, PASSES * PACK * V // STRIPE], U16, name="lists")
-        groups = [(0, 1)] + [(l,) for l in range(2, PASSES * PACK)]
+        groups = [(0, 1), (2, 3), (4, 5), (6, 7)]
         loaded = [keep.tile([P, len(group), T], F32, name=f"levels{group[0]}") for group in groups]
         tables = {l: tile[:, i, :] for group, tile in zip(groups, loaded) for i, l in enumerate(group)}
         w_codes = [keep.tile([P, N], U32, name=f"w_codes{a}", align_bytes=64) for a in range(PASSES)]
         w_bytes = keep.tile([P, N], U8, name="w_bytes", align_bytes=64)
-        x_rows = [keep.tile([P, V, PACK], BF16, name=f"x_rows{a}", align_bytes=64) for a in range(PASSES)]
+        x_rows = [[keep.tile([P, H, PACK], BF16, name=f"x_rows{a}_{h}", align_bytes=64) for h in range(2)] for a in range(PASSES)]
         x_codes = [keep.tile([P, V], U32, name=f"x_codes{a}", align_bytes=64) for a in range(PASSES)]
         x_bytes = [keep.tile([P, V], U8, name=f"x_bytes{a}", align_bytes=64) for a in range(PASSES)]
         warm = keep.tile([P, 8], F32, name="warm")
@@ -75,51 +74,52 @@ def tile_picked_grid_lin_relu_sub_l_kernel(tc, xT, w_words, w_scales, b, offs, o
 
         load_group(0)
         nc.sync.dma_start(out=lists[:], in_=offs)
-        for i in range(1, len(groups) - 2):
-            load_group(i)
+        load_group(1)
+        load_group(2)
         load_scales(0, 1)
-        load_group(len(groups) - 2)
-        load_scales(1, 2)
-        load_group(len(groups) - 1)
-        load_scales(2, 4)
+        load_group(3)
+        load_scales(1, 4)
         load_w(0, 0, N // 2)
         load_w(0, N // 2, N)
-        load_w(1, N // 2, N)
         load_w(1, 0, N // 2)
+        load_w(1, N // 2, N)
 
         nc.scalar.activation(warm_out[:], warm[:], COPY)
         make_identity(nc, ident[:], nomemset=True)
-        turned = psum.tile([P, P], F32, name="turned")
+        turned = psum.tile([P, P], F32, name="turned", tag="bank3_1")
         nc.tensor.transpose(turned[:], b_rows[:], ident[:])
 
-        rounded = {}
+        planes = [[keep.tile([P, PACK, H], F32, name=f"planes{a}_{h}") for h in range(2)] for a in range(PASSES)]
         accs = {}
 
         def picked(l, window, v0, v1):
             return window.indirect(lists[:, (l * V + v0) // STRIPE : (l * V + v1) // STRIPE])
 
-        def cast(l, engine_copy):
-            rounded[l] = keep.tile([P, T], BF16, name=f"half{l}")
-            engine_copy(rounded[l][:], tables[l])
+        def gather(l, h):
+            plane = planes[l // PACK][h][:, l % PACK, :]
+            if l % 2 == 0 or (l, h) == (5, 1):
+                nc.scalar.activation(plane, picked(l, tables[l], *HALVES[h]), COPY)
+            else:
+                nc.vector.tensor_copy(plane, picked(l, tables[l], *HALVES[h]))
 
-        def by_scalar(l, v0=0, v1=V):
-            nc.scalar.activation(x_rows[l // PACK][:, v0:v1, l % PACK], picked(l, rounded[l][:], v0, v1), COPY)
-
-        def by_vector(l, v0=0, v1=V):
-            nc.vector.tensor_copy(x_rows[l // PACK][:, v0:v1, l % PACK], picked(l, tables[l], v0, v1))
+        def weave(a, h):
+            nc.vector.tensor_copy(
+                x_rows[a][h][:].rearrange("p (c i) r -> p c r i", i=PACK),
+                planes[a][h][:].rearrange("p r (c i) -> p c r i", i=PACK),
+            )
 
         def quantise(a, v0, v1):
             nc.vector.quantize_mx(
                 out=x_codes[a][:, v0:v1].bitcast(FP8X4),
                 scales=x_bytes[a][:, v0:v1],
-                in_=x_rows[a][:, v0:v1, :].rearrange("p v r -> p (v r)"),
+                in_=x_rows[a][v0 // H][:].rearrange("p v r -> p (v r)"),
             )
 
         def multiply(a, c, h):
             cols = slice(c * P, (c + 1) * P)
             points = slice(*HALVES[h])
             if a == 0:
-                bank = f"bank{c}_0" if c >= 2 else f"bank{c}_{h}"
+                bank = f"bank{c}_{h}"
                 accs[c, h] = psum.tile([P, H], F32, name=f"acc{c}_{h}", tag=bank)
             nc.tensor.matmul_mx(
                 out=accs[c, h][:],
@@ -131,28 +131,14 @@ def tile_picked_grid_lin_relu_sub_l_kernel(tc, xT, w_words, w_scales, b, offs, o
                 stop=(a == PASSES - 1),
             )
 
-        cast(0, nc.vector.tensor_copy)
-        cast(1, nc.vector.tensor_copy)
-        by_scalar(0)
-        for v0, v1 in HALVES:
-            by_scalar(1, v0, v1)
-        by_vector(2)
-        for v0, v1 in HALVES:
-            by_vector(3, v0, v1)
-        for v0, v1 in HALVES:
-            quantise(0, v0, v1)
-
-        cast(4, nc.scalar.copy)
-        cast(5, nc.vector.tensor_copy)
-        for v0, v1 in HALVES:
-            by_scalar(4, v0, v1)
-            by_scalar(5, v0, v1)
-        by_vector(6)
-        by_vector(7, 0, H)
-        by_vector(7, H, H + QUARTER)
-        quantise(1, 0, H)
-        by_vector(7, H + QUARTER, V)
-        quantise(1, H, V)
+        for a in range(PASSES):
+            for l in range(a * PACK, (a + 1) * PACK):
+                for h in range(2):
+                    gather(l, h)
+            for h in range(2):
+                weave(a, h)
+            for v0, v1 in HALVES:
+                quantise(a, v0, v1)
 
         b_cols = keep.tile([P, M_TILES], F32, name="b_cols")
         nc.vector.tensor_copy(b_cols[:], turned[:, P - M_TILES :])
@@ -172,19 +158,15 @@ def tile_picked_grid_lin_relu_sub_l_kernel(tc, xT, w_words, w_scales, b, offs, o
         def store(c, v0, v1):
             nc.sync.dma_start(out=out_tiles[:, c : c + 1, v0:v1], in_=results[:, c : c + 1, v0:v1])
 
-        for h in range(2):
-            for c in (0, 1):
-                multiply(0, c, h)
-        for c in (2, 3):
-            multiply(0, c, 0)
-        for c in (2, 3):
-            close(c, 0)
-            store(c, 0, H)
-        for c in (0, 1):
+        for first in (0, 2):
+            for h in range(2):
+                for c in (first, first + 1):
+                    multiply(0, c, h)
+        close(0, 0)
+        store(0, 0, H)
+        for c in range(1, M_TILES):
             for h in range(2):
                 close(c, h)
             store(c, 0, V)
-        for c in (2, 3):
-            multiply(0, c, 1)
-            close(c, 1)
-            store(c, H, V)
+        close(0, 1)
+        store(0, H, V)

@@ -37,7 +37,7 @@ def tile_picked_grid_lin_relu_sub_l_kernel(tc, xT, w_words, w_scales, b, offs, o
         psum = ctx.enter_context(tc.psum_pool(name="psum", bufs=1))
 
         lists = keep.tile([P, PASSES * PACK * V // STRIPE], U16, name="lists")
-        groups = [(0, 1), (2, 3), (4, 5), (6, 7)]
+        groups = [(0, 1), (2, 3), (4,), (5,), (6,), (7,)]
         loaded = [keep.tile([P, len(group), T], F32, name=f"levels{group[0]}") for group in groups]
         tables = {l: tile[:, i, :] for group, tile in zip(groups, loaded) for i, l in enumerate(group)}
         w_codes = [keep.tile([P, N], U32, name=f"w_codes{a}", align_bytes=64) for a in range(PASSES)]
@@ -75,10 +75,10 @@ def tile_picked_grid_lin_relu_sub_l_kernel(tc, xT, w_words, w_scales, b, offs, o
         load_group(0)
         nc.sync.dma_start(out=lists[:], in_=offs)
         load_group(1)
-        load_group(2)
-        load_scales(0, 1)
-        load_group(3)
-        load_scales(1, 4)
+        load_scales(0, 2)
+        for i in range(2, len(groups)):
+            load_group(i)
+        load_scales(2, 4)
         load_w(0, 0, N // 2)
         load_w(0, N // 2, N)
         load_w(1, 0, N // 2)
@@ -89,23 +89,25 @@ def tile_picked_grid_lin_relu_sub_l_kernel(tc, xT, w_words, w_scales, b, offs, o
         turned = psum.tile([P, P], F32, name="turned", tag="bank3_1")
         nc.tensor.transpose(turned[:], b_rows[:], ident[:])
 
-        planes = [[keep.tile([P, PACK, H], F32, name=f"planes{a}_{h}") for h in range(2)] for a in range(PASSES)]
+        planes = [keep.tile([P, PACK, V], F32, name=f"planes{a}") for a in range(PASSES)]
         accs = {}
 
         def picked(l, window, v0, v1):
             return window.indirect(lists[:, (l * V + v0) // STRIPE : (l * V + v1) // STRIPE])
 
-        def gather(l, h):
-            plane = planes[l // PACK][h][:, l % PACK, :]
-            if l % 2 == 0 or (l, h) == (5, 1):
-                nc.scalar.activation(plane, picked(l, tables[l], *HALVES[h]), COPY)
-            else:
-                nc.vector.tensor_copy(plane, picked(l, tables[l], *HALVES[h]))
+        def piece(l, v0, v1):
+            return planes[l // PACK][:, l % PACK, v0:v1], picked(l, tables[l], v0, v1)
+
+        def by_scalar(l, v0, v1):
+            nc.scalar.activation(*piece(l, v0, v1), COPY)
+
+        def by_vector(l, v0, v1):
+            nc.vector.tensor_copy(*piece(l, v0, v1))
 
         def weave(a, h):
             nc.vector.tensor_copy(
                 x_rows[a][h][:].rearrange("p (c i) r -> p c r i", i=PACK),
-                planes[a][h][:].rearrange("p r (c i) -> p c r i", i=PACK),
+                planes[a][:, :, slice(*HALVES[h])].rearrange("p r (c i) -> p c r i", i=PACK),
             )
 
         def quantise(a, v0, v1):
@@ -131,14 +133,26 @@ def tile_picked_grid_lin_relu_sub_l_kernel(tc, xT, w_words, w_scales, b, offs, o
                 stop=(a == PASSES - 1),
             )
 
-        for a in range(PASSES):
-            for l in range(a * PACK, (a + 1) * PACK):
-                for h in range(2):
-                    gather(l, h)
+        def finish(a):
             for h in range(2):
                 weave(a, h)
             for v0, v1 in HALVES:
                 quantise(a, v0, v1)
+
+        by_scalar(0, 0, V)
+        by_vector(1, 0, V)
+        for v0, v1 in HALVES:
+            by_scalar(2, v0, v1)
+            by_vector(3, v0, v1)
+        finish(0)
+        by_scalar(4, 0, V)
+        by_scalar(5, 0, V)
+        by_vector(6, 0, V - H // 2)
+        by_scalar(6, V - H // 2, V)
+        for v0, v1 in HALVES:
+            by_vector(7, v0, v0 + H // 2)
+            by_scalar(7, v0 + H // 2, v1)
+        finish(1)
 
         b_cols = keep.tile([P, M_TILES], F32, name="b_cols")
         nc.vector.tensor_copy(b_cols[:], turned[:, P - M_TILES :])

@@ -106,8 +106,8 @@ def tile_picked_grid_lin_relu_sub_l_kernel(tc, xT, w_words, w_scales, b, offs, o
 
         def weave(a, h):
             nc.vector.tensor_copy(
-                x_rows[a][h][:].rearrange("p (c i) r -> p c r i", i=PACK),
-                planes[a][:, :, slice(*HALVES[h])].rearrange("p r (c i) -> p c r i", i=PACK),
+                x_rows[a][h][:].rearrange("p (c i) r -> p c r i", i=2),
+                planes[a][:, :, slice(*HALVES[h])].rearrange("p r (c i) -> p c r i", i=2),
             )
 
         def quantise(a, v0, v1):

@@ -81,12 +81,12 @@ def tile_picked_grid_lin_relu_sub_l_kernel(tc, xT, w_words, w_scales, b, offs, o
         load_scales(2, 4)
         load_w(0, 0, N // 2)
         load_w(0, N // 2, N)
-        load_w(1, 0, N // 2)
         load_w(1, N // 2, N)
+        load_w(1, 0, N // 2)
 
         nc.scalar.activation(warm_out[:], warm[:], COPY)
         make_identity(nc, ident[:], nomemset=True)
-        turned = psum.tile([P, P], F32, name="turned", tag="bank3_1")
+        turned = psum.tile([P, P], F32, name="turned")
         nc.tensor.transpose(turned[:], b_rows[:], ident[:])
 
         planes = [keep.tile([P, PACK, V], F32, name=f"planes{a}") for a in range(PASSES)]
@@ -121,7 +121,7 @@ def tile_picked_grid_lin_relu_sub_l_kernel(tc, xT, w_words, w_scales, b, offs, o
             cols = slice(c * P, (c + 1) * P)
             points = slice(*HALVES[h])
             if a == 0:
-                bank = f"bank{c}_{h}"
+                bank = f"bank{c}_0" if c == 3 else f"bank{c}_{h}"
                 accs[c, h] = psum.tile([P, H], F32, name=f"acc{c}_{h}", tag=bank)
             nc.tensor.matmul_mx(
                 out=accs[c, h][:],
@@ -172,15 +172,16 @@ def tile_picked_grid_lin_relu_sub_l_kernel(tc, xT, w_words, w_scales, b, offs, o
         def store(c, v0, v1):
             nc.sync.dma_start(out=out_tiles[:, c : c + 1, v0:v1], in_=results[:, c : c + 1, v0:v1])
 
-        for first in (0, 2):
+        for c in range(M_TILES - 1):
             for h in range(2):
-                for c in (first, first + 1):
-                    multiply(0, c, h)
-        close(0, 0)
-        store(0, 0, H)
-        for c in range(1, M_TILES):
+                multiply(0, c, h)
+        multiply(0, 3, 0)
+        close(3, 0)
+        store(3, 0, H)
+        for c in (2, 0, 1):
             for h in range(2):
                 close(c, h)
             store(c, 0, V)
-        close(0, 1)
-        store(0, H, V)
+        multiply(0, 3, 1)
+        close(3, 1)
+        store(3, H, V)

@@ -37,10 +37,11 @@ def tile_picked_grid_lin_relu_sub_l_kernel(tc, xT, w_words, w_scales, b, offs, o
         psum = ctx.enter_context(tc.psum_pool(name="psum", bufs=1))
 
         lists = keep.tile([P, PASSES * PACK * V // STRIPE], U16, name="lists")
-        groups = [(0, 1), (2, 3), (4,), (5,), (6,), (7,)]
+        groups = [(0,), (1, 2), (3,), (4,), (5,), (6,), (7,)]
         loaded = [keep.tile([P, len(group), T], F32, name=f"levels{group[0]}") for group in groups]
         tables = {l: tile[:, i, :] for group, tile in zip(groups, loaded) for i, l in enumerate(group)}
-        w_codes = [keep.tile([P, N], U32, name=f"w_codes{a}", align_bytes=64) for a in range(PASSES)]
+        w_both = keep.tile([P, PASSES, N], U32, name="w_both", align_bytes=64)
+        w_codes = [w_both[:, a, :] for a in range(PASSES)]
         w_bytes = keep.tile([P, N], U8, name="w_bytes", align_bytes=64)
         x_rows = [[keep.tile([P, H, PACK], BF16, name=f"x_rows{a}_{h}", align_bytes=64) for h in range(2)] for a in range(PASSES)]
         x_codes = [keep.tile([P, V], U32, name=f"x_codes{a}", align_bytes=64) for a in range(PASSES)]
@@ -75,14 +76,18 @@ def tile_picked_grid_lin_relu_sub_l_kernel(tc, xT, w_words, w_scales, b, offs, o
         load_group(0)
         nc.sync.dma_start(out=lists[:], in_=offs)
         load_group(1)
+        load_group(2)
         load_scales(0, 2)
-        for i in range(2, len(groups)):
+        for i in range(3, len(groups)):
             load_group(i)
         load_scales(2, 4)
-        load_w(0, 0, N // 2)
-        load_w(0, N // 2, N)
-        load_w(1, N // 2, N)
-        load_w(1, 0, N // 2)
+        load_w(0, 0, P)
+        load_w(0, P, N - P)
+        nc.sync.dma_start(
+            out=w_both[:, :, N - P :].bitcast(I32),
+            in_=w_words.rearrange("a p n r -> p a (n r)").bitcast(I32)[:, :, N - P :],
+        )
+        load_w(1, 0, N - P)
 
         nc.scalar.activation(warm_out[:], warm[:], COPY)
         make_identity(nc, ident[:], nomemset=True)
@@ -141,18 +146,25 @@ def tile_picked_grid_lin_relu_sub_l_kernel(tc, xT, w_words, w_scales, b, offs, o
 
         by_scalar(0, 0, V)
         by_vector(1, 0, V)
-        for v0, v1 in HALVES:
-            by_scalar(2, v0, v1)
-            by_vector(3, v0, v1)
+        by_scalar(2, 0, V)
+        by_scalar(3, 0, H)
+        by_vector(3, H, V)
         finish(0)
         by_scalar(4, 0, V)
-        by_scalar(5, 0, V)
-        by_vector(6, 0, V - H // 2)
-        by_scalar(6, V - H // 2, V)
         for v0, v1 in HALVES:
-            by_vector(7, v0, v0 + H // 2)
-            by_scalar(7, v0 + H // 2, v1)
-        finish(1)
+            by_scalar(5, v0, v1)
+        nc.vector.tensor_copy(
+            x_rows[1][0][:, :, :2].rearrange("p (c i) r -> p c r i", i=2),
+            planes[1][:, :2, :H].rearrange("p r (c i) -> p c r i", i=2),
+        )
+        nc.vector.tensor_copy(x_rows[1][0][:, :, 2], picked(6, tables[6], 0, H))
+        by_scalar(6, H, V)
+        by_vector(7, H, H + H // 2)
+        by_scalar(7, H + H // 2, V)
+        nc.vector.tensor_copy(x_rows[1][0][:, :, 3], picked(7, tables[7], 0, H))
+        weave(1, 1)
+        for v0, v1 in HALVES:
+            quantise(1, v0, v1)
 
         b_cols = keep.tile([P, M_TILES], F32, name="b_cols")
         nc.vector.tensor_copy(b_cols[:], turned[:, P - M_TILES :])

@@ -37,7 +37,7 @@ def tile_picked_grid_lin_relu_sub_l_kernel(tc, xT, w_words, w_scales, b, offs, o
         psum = ctx.enter_context(tc.psum_pool(name="psum", bufs=1))
 
         lists = keep.tile([P, PASSES * PACK * V // STRIPE], U16, name="lists")
-        groups = [(0,), (1, 2), (3,), (4,), (5,), (6,), (7,)]
+        groups = [(0, 1), (2,), (3,), (4,), (5,), (6,), (7,)]
         loaded = [keep.tile([P, len(group), T], F32, name=f"levels{group[0]}") for group in groups]
         tables = {l: tile[:, i, :] for group, tile in zip(groups, loaded) for i, l in enumerate(group)}
         w_both = keep.tile([P, PASSES, N], U32, name="w_both", align_bytes=64)
@@ -146,9 +146,9 @@ def tile_picked_grid_lin_relu_sub_l_kernel(tc, xT, w_words, w_scales, b, offs, o
 
         by_scalar(0, 0, V)
         by_vector(1, 0, V)
-        by_scalar(2, 0, V)
-        by_scalar(3, 0, H)
-        by_vector(3, H, V)
+        for l in (2, 3):
+            by_vector(l, 0, H)
+            by_scalar(l, H, V)
         finish(0)
         by_scalar(4, 0, V)
         for v0, v1 in HALVES:
@@ -166,7 +166,7 @@ def tile_picked_grid_lin_relu_sub_l_kernel(tc, xT, w_words, w_scales, b, offs, o
         for v0, v1 in HALVES:
             quantise(1, v0, v1)
 
-        b_cols = keep.tile([P, M_TILES], F32, name="b_cols")
+        b_cols = keep.tile([P, M_TILES], F32, name="b_cols", tag="x_rows1_0", align_bytes=64)
         nc.vector.tensor_copy(b_cols[:], turned[:, P - M_TILES :])
         results = keep.tile([P, M_TILES, V], F32, name="results")
         out_tiles = out.rearrange("(c p) v -> p c v", p=P)

from contextlib import ExitStack

import concourse.mybir as mybir
from concourse.masks import make_identity

F32 = mybir.dt.float32
BF16 = mybir.dt.bfloat16
I32 = mybir.dt.int32
U32 = mybir.dt.uint32
U16 = mybir.dt.uint16
U8 = mybir.dt.uint8
FP8X4 = mybir.dt.float8_e4m3fn_x4
COPY = mybir.ActivationFunctionType.Copy
RELU = mybir.ActivationFunctionType.Relu
ADD = mybir.AluOpType.add
MAX = mybir.AluOpType.max

P = 128
T = 512
V = 256
H = V // 2
N = 512
PASSES = 2
PACK = 4
M_TILES = N // P
STRIPE = 16
QUADRANT = 32
SCALE_ROWS = 4
HALVES = ((0, H), (H, V))
FLOPS = 2 * PASSES * P * PACK * N * V


def tile_picked_grid_lin_relu_sub_l_kernel(tc, xT, w_words, w_scales, b, offs, out):
    nc = tc.nc
    with ExitStack() as ctx:
        keep = ctx.enter_context(tc.tile_pool(name="keep", bufs=1))
        psum = ctx.enter_context(tc.psum_pool(name="psum", bufs=1))

        lists = keep.tile([P, PASSES * PACK * V // STRIPE], U16, name="lists")
        groups = [(0, 1), (2,), (3,), (4,), (5,), (6,), (7,)]
        loaded = [keep.tile([P, len(group), T], F32, name=f"levels{group[0]}") for group in groups]
        tables = {l: tile[:, i, :] for group, tile in zip(groups, loaded) for i, l in enumerate(group)}
        w_both = keep.tile([P, PASSES, N], U32, name="w_both", align_bytes=64)
        w_codes = [w_both[:, a, :] for a in range(PASSES)]
        w_bytes = keep.tile([P, N], U8, name="w_bytes", align_bytes=64)
        x_rows = [[keep.tile([P, H, PACK], BF16, name=f"x_rows{a}_{h}", align_bytes=64) for h in range(2)] for a in range(PASSES)]
        x_codes = [keep.tile([P, V], U32, name=f"x_codes{a}", align_bytes=64) for a in range(PASSES)]
        x_bytes = [keep.tile([P, V], U8, name=f"x_bytes{a}", align_bytes=64) for a in range(PASSES)]
        warm = keep.tile([P, 8], F32, name="warm")
        warm_out = keep.tile([P, 8], F32, name="warm_out")
        ident = keep.tile([P, P], F32, name="ident")
        b_rows = keep.tile([P, P], F32, name="b_rows")

        levels = xT.rearrange("(a f r) w -> a f r w", a=PASSES, r=PACK)

        nc.scalar.dma_start(out=b_rows[P - M_TILES :, :], in_=b.rearrange("(c p) o -> c (p o)", p=P))
        nc.gpsimd.memset(w_bytes[:].bitcast(U32), 0)
        nc.vector.memset(warm[:], 0.0)
        nc.vector.memset(ident[:], 0.0)
        nc.vector.memset(b_rows[: P - M_TILES, :], 0.0)

        def load_scales(q0, q1):
            for q in range(q0, q1):
                nc.sync.dma_start(
                    out=w_bytes[QUADRANT * q : QUADRANT * q + PASSES * SCALE_ROWS, :].bitcast(I32),
                    in_=w_scales[:, SCALE_ROWS * q : SCALE_ROWS * (q + 1), :].bitcast(I32),
                )

        def load_group(i):
            first, last = groups[i][0], groups[i][-1]
            nc.sync.dma_start(out=loaded[i][:], in_=levels[first // PACK, :, first % PACK : last % PACK + 1, :])

        def load_w(a, m0, m1):
            nc.sync.dma_start(out=w_codes[a][:, m0:m1].bitcast(I32), in_=w_words[a].rearrange("p n r -> p (n r)").bitcast(I32)[:, m0:m1])

        load_group(0)
        nc.sync.dma_start(out=lists[:], in_=offs)
        load_group(1)
        load_group(2)
        load_scales(0, 2)
        for i in range(3, len(groups)):
            load_group(i)
        load_scales(2, 4)
        load_w(0, 0, P)
        load_w(0, P, N - P)
        nc.sync.dma_start(
            out=w_both[:, :, N - P :].bitcast(I32),
            in_=w_words.rearrange("a p n r -> p a (n r)").bitcast(I32)[:, :, N - P :],
        )
        load_w(1, 0, N - P)

        nc.scalar.activation(warm_out[:], warm[:], COPY)
        make_identity(nc, ident[:], nomemset=True)
        turned = psum.tile([P, P], F32, name="turned")
        nc.tensor.transpose(turned[:], b_rows[:], ident[:])

        planes = [keep.tile([P, PACK, V], F32, name=f"planes{a}") for a in range(PASSES)]
        accs = {}

        def picked(l, window, v0, v1):
            return window.indirect(lists[:, (l * V + v0) // STRIPE : (l * V + v1) // STRIPE])

        def piece(l, v0, v1):
            return planes[l // PACK][:, l % PACK, v0:v1], picked(l, tables[l], v0, v1)

        def by_scalar(l, v0, v1):
            nc.scalar.activation(*piece(l, v0, v1), COPY)

        def by_vector(l, v0, v1):
            nc.vector.tensor_copy(*piece(l, v0, v1))

        def weave(a, h):
            nc.vector.tensor_copy(
                x_rows[a][h][:].rearrange("p (c i) r -> p c r i", i=2),
                planes[a][:, :, slice(*HALVES[h])].rearrange("p r (c i) -> p c r i", i=2),
            )

        def quantise(a, v0, v1):
            nc.vector.quantize_mx(
                out=x_codes[a][:, v0:v1].bitcast(FP8X4),
                scales=x_bytes[a][:, v0:v1],
                in_=x_rows[a][v0 // H][:].rearrange("p v r -> p (v r)"),
            )

        def multiply(a, c, h):
            cols = slice(c * P, (c + 1) * P)
            points = slice(*HALVES[h])
            if a == 0:
                bank = f"bank{c}_0" if c == 3 else f"bank{c}_{h}"
                accs[c, h] = psum.tile([P, H], F32, name=f"acc{c}_{h}", tag=bank)
            nc.tensor.matmul_mx(
                out=accs[c, h][:],
                lhsT=w_codes[a][:, cols].bitcast(FP8X4),
                lhsT_scale=w_bytes[SCALE_ROWS * a :, cols],
                rhs=x_codes[a][:, points].bitcast(FP8X4),
                rhs_scale=x_bytes[a][:, points],
                start=(a == 0),
                stop=(a == PASSES - 1),
            )

        def finish(a):
            for h in range(2):
                weave(a, h)
            for v0, v1 in HALVES:
                quantise(a, v0, v1)

        by_scalar(0, 0, V)
        by_vector(1, 0, V)
        for l in (2, 3):
            by_vector(l, 0, H)
            by_scalar(l, H, V)
        finish(0)
        by_scalar(4, 0, V)
        for v0, v1 in HALVES:
            by_scalar(5, v0, v1)
        nc.vector.tensor_copy(
            x_rows[1][0][:, :, :2].rearrange("p (c i) r -> p c r i", i=2),
            planes[1][:, :2, :H].rearrange("p r (c i) -> p c r i", i=2),
        )
        nc.vector.tensor_copy(x_rows[1][0][:, :, 2], picked(6, tables[6], 0, H))
        by_scalar(6, H, V)
        by_vector(7, H, H + H // 2)
        by_scalar(7, H + H // 2, V)
        nc.vector.tensor_copy(x_rows[1][0][:, :, 3], picked(7, tables[7], 0, H))
        weave(1, 1)
        for v0, v1 in HALVES:
            quantise(1, v0, v1)

        b_cols = keep.tile([P, M_TILES], F32, name="b_cols", tag="x_rows1_0", align_bytes=64)
        nc.vector.tensor_copy(b_cols[:], turned[:, P - M_TILES :])
        results = keep.tile([P, M_TILES, V], F32, name="results")
        out_tiles = out.rearrange("(c p) v -> p c v", p=P)
        closed = []

        def close(c, h):
            v0, v1 = HALVES[h]
            multiply(1, c, h)
            if len(closed) % 2 == 0:
                nc.scalar.activation(results[:, c, v0:v1], accs[c, h][:], RELU, bias=b_cols[:, c : c + 1])
            else:
                nc.vector.tensor_scalar(results[:, c, v0:v1], accs[c, h][:], b_cols[:, c : c + 1], 0.0, ADD, MAX)
            closed.append((c, h))

        def store(c, v0, v1):
            nc.sync.dma_start(out=out_tiles[:, c : c + 1, v0:v1], in_=results[:, c : c + 1, v0:v1])

        for c in range(M_TILES - 1):
            for h in range(2):
                multiply(0, c, h)
        multiply(0, 3, 0)
        close(3, 0)
        store(3, 0, H)
        for c in (2, 0, 1):
            for h in range(2):
                close(c, h)
            store(c, 0, V)
        multiply(0, 3, 1)
        close(3, 1)
        store(3, H, V)
